import numpy as np
import ml_dtypes


def mxq(x, axis, fmt="e4m3"):
    dtype, down = {"e4m3": (ml_dtypes.float8_e4m3fn, 7), "e5m2": (ml_dtypes.float8_e5m2, 14)}[fmt]
    v = np.moveaxis(np.asarray(x, np.float32).astype(ml_dtypes.bfloat16).astype(np.float64), axis, -1)
    blocks = v.reshape(v.shape[:-1] + (-1, 32))
    amax = np.abs(blocks).max(-1, keepdims=True)
    byte = np.maximum(np.where(amax > 0, np.frexp(amax)[1] - 1 + 127, 0) - down, 1)
    scale = np.exp2(byte - 127.0)
    codes = (blocks / scale).astype(np.float32).astype(dtype).astype(np.float64)
    return np.moveaxis((codes * scale).reshape(v.shape), -1, axis)


WIDE = False


def mx_kscale(k):
    if not WIDE:
        return np.ones(k)
    levels = np.array([10, -10, 5, -5, 0])
    if k % 512:
        return np.exp2(np.random.permutation(np.resize(levels, k // 32))).repeat(32)
    a = np.empty((k // 512, 16))
    for p in range(k // 512):
        a[p, :8] = np.random.permutation(np.resize(levels, 8))
        for g in range(8):
            far = levels[np.abs(levels - a[p, g]) >= 10]
            a[p, g + 8] = far[np.random.randint(len(far))]
    return np.exp2(a.ravel()).repeat(32)


BF16 = ml_dtypes.bfloat16


def bf(x):
    return np.asarray(x, np.float32).astype(BF16)


def f64(x):
    return np.asarray(x).astype(np.float64)


E2M1 = np.array([0.0, 0.5, 1.0, 1.5, 2.0, 3.0, 4.0, 6.0, -0.0, -0.5, -1.0, -1.5, -2.0, -3.0, -4.0, -6.0])


def pack_weight(w, fmt):
    k, n = w.shape
    w = f64(bf(w)).reshape(k // 32, 32, n)
    amax = np.abs(w).max(1)
    if fmt == "e4m3":
        byte = np.frexp(amax)[1] - 1 + 127 - 7
    else:
        mant, ex = np.frexp(amax / 6.0)
        byte = np.where(mant > 0.5, ex, ex - 1) + 127
    byte = np.clip(np.where(amax > 0, byte, 1), 1, 254)
    scaled = (w * np.exp2(127.0 - byte)[:, None, :]).reshape(k, n).astype(np.float32)
    by_word = np.ascontiguousarray(scaled.reshape(k // 512, 128, 4, n).transpose(0, 1, 3, 2))
    if fmt == "e4m3":
        words = by_word.astype(ml_dtypes.float8_e4m3fn).view(np.uint8)
    else:
        c = by_word.astype(ml_dtypes.float4_e2m1fn).view(np.uint8) & 0xF
        words = c[..., 0::2] | (c[..., 1::2] << 4)
    return np.ascontiguousarray(words), np.ascontiguousarray(byte.astype(np.uint8).reshape(k // 512, 16, n))


def unpack_weight(words, scales, fmt):
    g, p, n, _ = words.shape
    if fmt == "e4m3":
        vals = np.ascontiguousarray(words).view(ml_dtypes.float8_e4m3fn).astype(np.float64)
    else:
        nib = np.empty((g, p, n, 4), np.uint8)
        nib[..., 0::2] = words & 0xF
        nib[..., 1::2] = words >> 4
        vals = E2M1[nib]
    vals = vals * np.repeat(np.exp2(scales.astype(np.float64) - 127.0), 8, axis=1)[..., None]
    return vals.transpose(0, 1, 3, 2).reshape(g * 512, n)
def pack4(w):
    words, scales = pack_weight(w, "e2m1")
    return words.reshape(words.shape[0], 128, -1), scales


def unpack4(words, scales):
    return unpack_weight(words.reshape(words.shape[0], 128, -1, 2), scales, "e2m1")


T, K, J, B, N = 1024, 2048, 512, 512, 1024

MAIN, AUX = 0.6, 0.5


def setup_inputs():
    s = mx_kscale(K)
    r = mx_kscale(J)
    x_main = bf(np.random.standard_normal((T, K)) * s)
    x_aux = bf(np.random.standard_normal((T, J)) * r)
    w_words, w_scales = pack4(MAIN * np.random.standard_normal((K, N)) / np.sqrt(K) / s[:, None])
    v = bf(AUX * np.random.standard_normal((J, N)) / np.sqrt(J) / r[:, None])
    inv_noise = bf(1 + 0.1 * np.random.standard_normal(B))
    return {"x_main": x_main, "x_aux": x_aux, "w_words": w_words, "w_scales": w_scales,
            "v": v, "inv_noise": inv_noise}


def reference(x_main, x_aux, w_words, w_scales, v, inv_noise):
    main = mxq(f64(x_main), 1, "e4m3") @ unpack4(w_words, w_scales)
    aux = mxq(f64(x_aux), 1, "e4m3") @ mxq(f64(v), 0, "e4m3")
    y = main + aux
    power = y[:, :B] ** 2 + y[:, B:] ** 2
    stat = power * f64(inv_noise)
    peak = stat.max(axis=1)
    return stat, peak

@@ -1,0 +1,293 @@
+from contextlib import ExitStack
+
+import concourse.mybir as mybir
+from concourse.masks import make_identity
+
+F32 = mybir.dt.float32
+BF16 = mybir.dt.bfloat16
+I32 = mybir.dt.int32
+U32 = mybir.dt.uint32
+U8 = mybir.dt.uint8
+FP8X4 = mybir.dt.float8_e4m3fn_x4
+FP4X4 = mybir.dt.float4_e2m1fn_x4
+ALU = mybir.AluOpType
+ACT = mybir.ActivationFunctionType
+AX = mybir.AxisListType
+
+P = 128
+T, K, J, B, N = 1024, 2048, 512, 512, 1024
+NT = T // P
+FLOPS = 2 * T * N * (K + J)
+PERM_ON_SCALAR = [(5, 1), (6, 1), (7, 1)]
+V_SPLIT = 320
+
+
+def tile_beamformer_detection_statistics_s1_kernel(
+    tc, x_main, x_aux, w_words, w_scales, v, inv_noise, stat_out, peak_out
+):
+    nc = tc.nc
+    xm = x_main.rearrange("(p i) k -> p i k", i=NT)
+    xa = x_aux.rearrange("(p i) k -> p i k", i=NT)
+    so = stat_out.rearrange("(p i) b -> p i b", i=NT)
+    po = peak_out.rearrange("(p i) -> p i", i=NT)
+
+    with ExitStack() as ctx:
+        keep = ctx.enter_context(tc.tile_pool(name="keep", bufs=1))
+        work = ctx.enter_context(tc.tile_pool(name="work", bufs=4))
+        epi = ctx.enter_context(tc.tile_pool(name="epi", bufs=4))
+        turn = ctx.enter_context(tc.psum_pool(name="turn", bufs=4))
+        accs = ctx.enter_context(tc.psum_pool(name="accs", bufs=2))
+
+        wsc = keep.tile([P, 4 * N], U8, align_bytes=64, name="wsc")
+        nc.vector.memset(wsc[:].bitcast(I32), 0)
+        warm = keep.tile([P, 2], F32, name="warm")
+        nc.vector.memset(warm[:], 1.0)
+        inv_row = keep.tile([P, B], BF16, align_bytes=64, name="inv_row")
+        nc.vector.memset(inv_row[:], 0.0)
+        ones = keep.tile([P, P], BF16, align_bytes=64, name="ones")
+        nc.vector.memset(ones[:], 1.0)
+        ident = keep.tile([P, P], F32, align_bytes=64, name="ident")
+        make_identity(nc, ident[:])
+        ctx.enter_context(tc.manual_schedule())
+
+        raws = {}
+
+        def load_main(i, split):
+            if split:
+                for h in (0, 1):
+                    r = keep.tile([P, 1024], BF16, align_bytes=64, name="raw%d_%d" % (i, h))
+                    nc.sync.dma_start(out=r[:], in_=xm[:, i, 1024 * h : 1024 * (h + 1)])
+                    raws[(i, h)] = r[:]
+            else:
+                r = keep.tile([P, 2048], BF16, align_bytes=64, name="raw%d" % i)
+                nc.sync.dma_start(out=r[:], in_=xm[:, i, :])
+                for h in (0, 1):
+                    raws[(i, h)] = r[:, 1024 * h : 1024 * (h + 1)]
+
+        def load_aux(i):
+            r = keep.tile([P, 2, J], BF16, align_bytes=64, name="rawa%d" % i)
+            nc.sync.dma_start(out=r[:], in_=xa[:, i : i + 2, :])
+            raws[(i, 2)] = r[:].rearrange("p s k -> p (s k)")
+
+        load_main(0, True)
+        load_main(1, False)
+        w_tiles = []
+
+        def load_w(c):
+            wt = keep.tile([P, 2, 2 * N], U8, align_bytes=64, name="w%d" % c)
+            nc.sync.dma_start(out=wt[:].bitcast(I32), in_=w_words[2 * c : 2 * c + 2].bitcast(I32).rearrange("g p b -> p g b"))
+            w_tiles.extend([wt[:, 0, :], wt[:, 1, :]])
+
+        load_w(0)
+        ws_i32 = w_scales.bitcast(I32)
+        for q in range(4):
+            nc.sync.dma_start(
+                out=wsc[32 * q : 32 * q + 4, :].bitcast(I32).rearrange("p (g n) -> p g n", g=4),
+                in_=ws_i32[:, 4 * q : 4 * q + 4, :].rearrange("g r n -> r g n"),
+            )
+        nc.gpsimd.dma_start(out=inv_row[0:1, :], in_=inv_noise.rearrange("(o b) -> o b", o=1))
+        nc.scalar.activation(warm[:, 1:2], warm[:, 0:1], ACT.Square)
+        load_w(1)
+        load_aux(0)
+        v_view = v.rearrange("(p j) n -> p j n", j=4)
+        v_raws = []
+        for h in (0, 1):
+            vr = keep.tile([P, 4, 512], BF16, align_bytes=64, name="vraw%d" % h)
+            nc.sync.dma_start(out=vr[:], in_=v_view[:, :, 512 * h : 512 * (h + 1)])
+            v_raws.append(vr)
+        for i in range(2, NT):
+            load_main(i, False)
+            if i % 2 == 1:
+                load_aux(i - 1)
+
+        xps, xts, grps, codes = {}, {}, {}, {}
+
+        def perm(u):
+            xp = work.tile([P, 2, 2, P], F32, align_bytes=64, name="xp", bufs=6)
+            copy = nc.scalar.copy if u in PERM_ON_SCALAR else nc.vector.tensor_copy
+            copy(out=xp[:], in_=raws[u].bitcast(F32).rearrange("p (s a u) -> p s u a", s=2, u=2))
+            xps[u] = xp
+
+        def trans(u):
+            xt = turn.tile([P, 2, 2, P], F32, name="xt")
+            for s in (0, 1):
+                for w in (0, 1):
+                    nc.tensor.transpose(xt[:, s, w, :], xps[u][:, s, w, :], ident[:])
+            xts[u] = xt
+
+        def drain(u):
+            grp = work.tile([P, 1024], BF16, align_bytes=64, name="grp", bufs=4)
+            nc.scalar.copy(
+                out=grp[:].bitcast(F32).rearrange("p (s r u) -> p s r u", s=2, u=2),
+                in_=xts[u][:].rearrange("p s u r -> p s r u"),
+            )
+            grps[u] = grp
+
+        def quant(u):
+            c = keep.tile([P, 256], U32, align_bytes=64, name="code%d_%d" % u)
+            sc = keep.tile([P, 256], U8, align_bytes=64, name="scale%d_%d" % u)
+            nc.vector.quantize_mx(out=c[:].bitcast(FP8X4), scales=sc[:], in_=grps[u][:])
+            codes[u] = (c, sc)
+
+        v_grps, v_codes = [], []
+        for h in (0, 1):
+            v_grps.append(keep.tile([P, 512, 4], BF16, align_bytes=64, name="vgrp%d" % h))
+            v_codes.append(
+                (
+                    keep.tile([P, 512], U32, align_bytes=64, name="vcode%d" % h),
+                    keep.tile([P, 512], U8, align_bytes=64, name="vscale%d" % h),
+                )
+            )
+
+        def v_inter(h):
+            src = v_raws[h][:].rearrange("p t n -> p n t")
+            nc.vector.tensor_copy(out=v_grps[h][:, 0:V_SPLIT, :], in_=src[:, 0:V_SPLIT, :])
+            nc.scalar.copy(out=v_grps[h][:, V_SPLIT:512, :], in_=src[:, V_SPLIT:512, :])
+
+        def v_quant(h):
+            c, sc = v_codes[h]
+            nc.vector.quantize_mx(
+                out=c[:].bitcast(FP8X4), scales=sc[:], in_=v_grps[h][:].rearrange("p n t -> p (n t)")
+            )
+
+        acc = {}
+
+        def mm_main(i, halves=(0, 1)):
+            if 0 in halves:
+                re = accs.tile([P, 512], F32, name="acc_re")
+                im = accs.tile([P, 512], F32, name="acc_im")
+                acc[i] = (re, im)
+            for g in range(4):
+                c, sc = codes[(i, g // 2)]
+                cols = slice(P * (g % 2), P * (g % 2) + P)
+                for h in halves:
+                    nc.tensor.matmul_mx(
+                        out=acc[i][h][:],
+                        lhsT=c[:, cols].bitcast(FP8X4),
+                        lhsT_scale=sc[:, cols],
+                        rhs=w_tiles[g][:, 1024 * h : 1024 * (h + 1)].bitcast(FP4X4),
+                        rhs_scale=wsc[:, N * g + 512 * h : N * g + 512 * (h + 1)],
+                        start=(g == 0),
+                        stop=False,
+                    )
+
+        def mm_aux(i, halves=(0, 1)):
+            c, sc = codes[(i - i % 2, 2)]
+            cols = slice(P * (i % 2), P * (i % 2) + P)
+            for h in halves:
+                vc, vs = v_codes[h]
+                nc.tensor.matmul_mx(
+                    out=acc[i][h][:],
+                    lhsT=c[:, cols].bitcast(FP8X4),
+                    lhsT_scale=sc[:, cols],
+                    rhs=vc[:].bitcast(FP8X4),
+                    rhs_scale=vs[:],
+                    start=False,
+                    stop=True,
+                )
+
+        sqs, sums, stats = {}, {}, {}
+        peaks = keep.tile([P, NT], F32, align_bytes=64, name="peaks")
+        inv = keep.tile([P, B], F32, align_bytes=64, name="inv")
+
+        def square(i, h):
+            sq = epi.tile([P, B], F32, name="sq%d" % h)
+            nc.scalar.activation(sq[:], acc[i][h][:], ACT.Square)
+            sqs[(i, h)] = sq
+
+        def f_add(i):
+            sm = epi.tile([P, B], F32, name="sm")
+            nc.vector.tensor_tensor(out=sm[:], in0=sqs[(i, 0)][:], in1=sqs[(i, 1)][:], op=ALU.add)
+            sums[i] = sm
+
+        def f_mul(i):
+            st = epi.tile([P, B], F32, name="st")
+            nc.vector.tensor_tensor(out=st[:], in0=sums[i][:], in1=inv[:], op=ALU.mult)
+            nc.sync.dma_start(out=so[:, i, :], in_=st[:])
+            stats[i] = st
+
+        def f_max(i):
+            nc.vector.tensor_reduce(out=peaks[:, i : i + 1], in_=stats[i][:], axis=AX.X, op=ALU.max)
+
+        head = [(0, 0), (0, 1), (1, 0), (1, 1)]
+        for u in head:
+            perm(u)
+        for u in head:
+            trans(u)
+            drain(u)
+            quant(u)
+        inv_ps = turn.tile([P, 2, 2, P], F32, name="xt")
+        nc.tensor.matmul(inv_ps[:].rearrange("p s u r -> p (s u r)"), lhsT=ones[:], rhs=inv_row[:], start=True, stop=True)
+        nc.scalar.copy(out=inv[:], in_=inv_ps[:].rearrange("p s u r -> p (s u r)"))
+        mm_main(0)
+        perm((0, 2))
+        trans((0, 2))
+        mm_main(1)
+        v_inter(0)
+        drain((0, 2))
+        v_inter(1)
+        for u in [(2, 0), (2, 1)]:
+            perm(u)
+        v_quant(0)
+        quant((0, 2))
+        v_quant(1)
+        for u in [(2, 0), (2, 1)]:
+            trans(u)
+            drain(u)
+        mm_aux(0)
+        mm_aux(1)
+        square(0, 0)
+        square(0, 1)
+        perm((3, 0))
+        perm((3, 1))
+        quant((2, 0))
+        perm((2, 2))
+        quant((2, 1))
+
+        def units(i):
+            if i >= NT:
+                return []
+            return [(i, 0), (i, 1)] + ([(i, 2)] if i % 2 == 0 else [])
+
+        finishes = {2: [0], 3: [1], 4: [2, 3], 5: [4], 6: [5], 7: [6]}
+        for i in range(2, NT):
+            turned = units(i + 1) if i > 2 else [(3, 0), (3, 1), (2, 2)]
+            for u in turned:
+                trans(u)
+            if i > 2:
+                square(i - 1, 0)
+                square(i - 1, 1)
+            for u in turned:
+                drain(u)
+            if i == 2:
+                square(1, 0)
+                square(1, 1)
+            a = [lambda u=u: perm(u) for u in units(i + 2)[:1]] + [lambda u=u: quant(u) for u in turned] + [lambda u=u: perm(u) for u in units(i + 2)[1:]]
+            b = [lambda f=f, j=j: f(j) for f in (f_add, f_mul, f_max) for j in finishes[i]]
+            for k in range(max(len(a), len(b))):
+                if k < len(a):
+                    a[k]()
+                if k < len(b):
+                    b[k]()
+            if i < NT - 1:
+                mm_main(i)
+                mm_aux(i)
+
+        last = NT - 1
+        for h in (0, 1):
+            mm_main(last, (h,))
+            mm_aux(last, (h,))
+        square(last, 0)
+        sq_im = epi.tile([P, B], F32, name="sq1")
+        sm = epi.tile([P, B], F32, name="sm")
+        st = epi.tile([P, B], F32, name="st")
+        cols = [slice(0, 256), slice(256, 512)]
+        for c in cols:
+            nc.scalar.activation(sq_im[:, c], acc[last][1][:, c], ACT.Square)
+        for c in cols:
+            nc.vector.tensor_tensor(out=sm[:, c], in0=sqs[(last, 0)][:, c], in1=sq_im[:, c], op=ALU.add)
+        for c in cols:
+            nc.vector.tensor_tensor(out=st[:, c], in0=sm[:, c], in1=inv[:, c], op=ALU.mult)
+            nc.sync.dma_start(out=so[:, last, c], in_=st[:, c])
+        nc.vector.tensor_reduce(out=peaks[:, last : last + 1], in_=st[:], axis=AX.X, op=ALU.max)
+        nc.sync.dma_start(out=po, in_=peaks[:])

@@ -40,12 +40,14 @@ def tile_beamformer_detection_statistics_s1_kernel(
 
         wsc = keep.tile([P, 4 * N], U8, align_bytes=64, name="wsc")
         nc.vector.memset(wsc[:].bitcast(I32), 0)
+        zeros = keep.tile([P, B], BF16, align_bytes=64, name="zeros")
+        nc.vector.memset(zeros[:], 0.0)
+        ones = keep.tile([P, P], BF16, align_bytes=64, name="ones")
+        nc.vector.memset(ones[:], 1.0)
         warm = keep.tile([P, 2], F32, name="warm")
         nc.vector.memset(warm[:], 1.0)
         inv_row = keep.tile([P, B], BF16, align_bytes=64, name="inv_row")
         nc.vector.memset(inv_row[:], 0.0)
-        ones = keep.tile([P, P], BF16, align_bytes=64, name="ones")
-        nc.vector.memset(ones[:], 1.0)
         ident = keep.tile([P, P], F32, align_bytes=64, name="ident")
         make_identity(nc, ident[:])
         ctx.enter_context(tc.manual_schedule())
@@ -70,7 +72,6 @@ def tile_beamformer_detection_statistics_s1_kernel(
             raws[(i, 2)] = r[:].rearrange("p s k -> p (s k)")
 
         load_main(0, True)
-        load_main(1, False)
         w_tiles = []
 
         def load_w(c):
@@ -78,15 +79,15 @@ def tile_beamformer_detection_statistics_s1_kernel(
             nc.sync.dma_start(out=wt[:].bitcast(I32), in_=w_words[2 * c : 2 * c + 2].bitcast(I32).rearrange("g p b -> p g b"))
             w_tiles.extend([wt[:, 0, :], wt[:, 1, :]])
 
-        load_w(0)
         ws_i32 = w_scales.bitcast(I32)
         for q in range(4):
             nc.sync.dma_start(
                 out=wsc[32 * q : 32 * q + 4, :].bitcast(I32).rearrange("p (g n) -> p g n", g=4),
                 in_=ws_i32[:, 4 * q : 4 * q + 4, :].rearrange("g r n -> r g n"),
             )
-        nc.gpsimd.dma_start(out=inv_row[0:1, :], in_=inv_noise.rearrange("(o b) -> o b", o=1))
         nc.scalar.activation(warm[:, 1:2], warm[:, 0:1], ACT.Square)
+        load_main(1, False)
+        load_w(0)
         load_w(1)
         load_aux(0)
         v_view = v.rearrange("(p j) n -> p j n", j=4)
@@ -95,6 +96,7 @@ def tile_beamformer_detection_statistics_s1_kernel(
             vr = keep.tile([P, 4, 512], BF16, align_bytes=64, name="vraw%d" % h)
             nc.sync.dma_start(out=vr[:], in_=v_view[:, :, 512 * h : 512 * (h + 1)])
             v_raws.append(vr)
+        nc.sync.dma_start(out=inv_row[0:1, :], in_=inv_noise.rearrange("(o b) -> o b", o=1))
         for i in range(2, NT):
             load_main(i, False)
             if i % 2 == 1:
@@ -195,20 +197,27 @@ def tile_beamformer_detection_statistics_s1_kernel(
             nc.scalar.activation(sq[:], acc[i][h][:], ACT.Square)
             sqs[(i, h)] = sq
 
-        def f_add(i):
-            sm = epi.tile([P, B], F32, name="sm")
-            nc.vector.tensor_tensor(out=sm[:], in0=sqs[(i, 0)][:], in1=sqs[(i, 1)][:], op=ALU.add)
-            sums[i] = sm
+        def f_add(i, c=slice(0, B)):
+            if i not in sums:
+                sums[i] = epi.tile([P, B], F32, name="sm")
+            nc.vector.tensor_tensor(out=sums[i][:, c], in0=sqs[(i, 0)][:, c], in1=sqs[(i, 1)][:, c], op=ALU.add)
 
-        def f_mul(i):
-            st = epi.tile([P, B], F32, name="st")
-            nc.vector.tensor_tensor(out=st[:], in0=sums[i][:], in1=inv[:], op=ALU.mult)
-            nc.sync.dma_start(out=so[:, i, :], in_=st[:])
-            stats[i] = st
+        def f_mul(i, c=slice(0, B)):
+            if i not in stats:
+                stats[i] = epi.tile([P, B], F32, name="st")
+            nc.vector.tensor_tensor(out=stats[i][:, c], in0=sums[i][:, c], in1=inv[:, c], op=ALU.mult)
+            if c.stop == B:
+                nc.sync.dma_start(out=so[:, i, :], in_=stats[i][:])
 
         def f_max(i):
             nc.vector.tensor_reduce(out=peaks[:, i : i + 1], in_=stats[i][:], axis=AX.X, op=ALU.max)
 
+        def dummies(n):
+            ps = turn.tile([P, 2, 2, P], F32, name="xt")
+            for k in range(n):
+                nc.tensor.matmul(ps[:].rearrange("p s u r -> p (s u r)"), lhsT=ones[:], rhs=zeros[:], start=True, stop=True)
+
+        dummies(4)
         head = [(0, 0), (0, 1), (1, 0), (1, 1)]
         for u in head:
             perm(u)
@@ -216,9 +225,8 @@ def tile_beamformer_detection_statistics_s1_kernel(
             trans(u)
             drain(u)
             quant(u)
-        inv_ps = turn.tile([P, 2, 2, P], F32, name="xt")
-        nc.tensor.matmul(inv_ps[:].rearrange("p s u r -> p (s u r)"), lhsT=ones[:], rhs=inv_row[:], start=True, stop=True)
-        nc.scalar.copy(out=inv[:], in_=inv_ps[:].rearrange("p s u r -> p (s u r)"))
+            if u[1] == 1:
+                dummies(1)
         mm_main(0)
         perm((0, 2))
         trans((0, 2))
@@ -231,6 +239,9 @@ def tile_beamformer_detection_statistics_s1_kernel(
         v_quant(0)
         quant((0, 2))
         v_quant(1)
+        inv_ps = turn.tile([P, 2, 2, P], F32, name="xt")
+        nc.tensor.matmul(inv_ps[:].rearrange("p s u r -> p (s u r)"), lhsT=ones[:], rhs=inv_row[:], start=True, stop=True)
+        nc.scalar.copy(out=inv[:], in_=inv_ps[:].rearrange("p s u r -> p (s u r)"))
         for u in [(2, 0), (2, 1)]:
             trans(u)
             drain(u)
@@ -244,14 +255,17 @@ def tile_beamformer_detection_statistics_s1_kernel(
         perm((2, 2))
         quant((2, 1))
 
-        def units(i):
-            if i >= NT:
-                return []
-            return [(i, 0), (i, 1)] + ([(i, 2)] if i % 2 == 0 else [])
-
+        turns = {
+            2: [(3, 0), (3, 1), (2, 2)],
+            3: [(4, 0), (4, 1), (4, 2)],
+            4: [(5, 0), (5, 1)],
+            5: [(6, 0), (6, 1), (6, 2)],
+            6: [(7, 0), (7, 1)],
+        }
         finishes = {2: [0], 3: [1], 4: [2, 3], 5: [4], 6: [5], 7: [6]}
         for i in range(2, NT):
-            turned = units(i + 1) if i > 2 else [(3, 0), (3, 1), (2, 2)]
+            turned = turns.get(i, [])
+            laid = turns.get(i + 1, [])
             for u in turned:
                 trans(u)
             if i > 2:
@@ -262,8 +276,13 @@ def tile_beamformer_detection_statistics_s1_kernel(
             if i == 2:
                 square(1, 0)
                 square(1, 1)
-            a = [lambda u=u: perm(u) for u in units(i + 2)[:1]] + [lambda u=u: quant(u) for u in turned] + [lambda u=u: perm(u) for u in units(i + 2)[1:]]
-            b = [lambda f=f, j=j: f(j) for f in (f_add, f_mul, f_max) for j in finishes[i]]
+            a = [lambda u=u: perm(u) for u in laid[:1]] + [lambda u=u: quant(u) for u in turned] + [lambda u=u: perm(u) for u in laid[1:]]
+            if i < 6:
+                b = [lambda f=f, j=j: f(j) for f in (f_add, f_mul, f_max) for j in finishes[i]]
+            else:
+                b = [lambda f=f, c=c: f(i - 1, c) for f in (f_add, f_mul) for c in (slice(0, 256), slice(256, B))]
+                if i == 6:
+                    b.append(lambda: f_max(i - 1))
             for k in range(max(len(a), len(b))):
                 if k < len(a):
                     a[k]()
@@ -274,20 +293,47 @@ def tile_beamformer_detection_statistics_s1_kernel(
                 mm_aux(i)
 
         last = NT - 1
-        for h in (0, 1):
-            mm_main(last, (h,))
-            mm_aux(last, (h,))
+        mm_main(last, (0,))
+        mm_aux(last, (0,))
         square(last, 0)
+        pieces = [slice(P * q, P * (q + 1)) for q in range(4)]
+        acc_im = acc[last][1]
+        for n in pieces:
+            for g in range(5):
+                c, sc = codes[(last, g // 2)] if g < 4 else codes[(last - 1, 2)]
+                cols = slice(P * (g % 2), P * (g % 2) + P) if g < 4 else slice(P, 2 * P)
+                w = w_tiles[g][:, 1024 + 2 * n.start : 1024 + 2 * n.stop].bitcast(FP4X4) if g < 4 else v_codes[1][0][:, n].bitcast(FP8X4)
+                ws = wsc[:, N * g + 512 + n.start : N * g + 512 + n.stop] if g < 4 else v_codes[1][1][:, n]
+                nc.tensor.matmul_mx(
+                    out=acc_im[:, n],
+                    lhsT=c[:, cols].bitcast(FP8X4),
+                    lhsT_scale=sc[:, cols],
+                    rhs=w,
+                    rhs_scale=ws,
+                    start=(g == 0),
+                    stop=(g == 4),
+                )
         sq_im = epi.tile([P, B], F32, name="sq1")
         sm = epi.tile([P, B], F32, name="sm")
-        st = epi.tile([P, B], F32, name="st")
-        cols = [slice(0, 256), slice(256, 512)]
-        for c in cols:
-            nc.scalar.activation(sq_im[:, c], acc[last][1][:, c], ACT.Square)
-        for c in cols:
+        st = epi.tile([P, B + 1], F32, name="stl", bufs=1)
+        spans = [slice(0, 256), slice(256, 384), slice(384, 512)]
+
+        def l_add(c):
             nc.vector.tensor_tensor(out=sm[:, c], in0=sqs[(last, 0)][:, c], in1=sq_im[:, c], op=ALU.add)
-        for c in cols:
+
+        def l_mul(c):
             nc.vector.tensor_tensor(out=st[:, c], in0=sm[:, c], in1=inv[:, c], op=ALU.mult)
             nc.sync.dma_start(out=so[:, last, c], in_=st[:, c])
-        nc.vector.tensor_reduce(out=peaks[:, last : last + 1], in_=st[:], axis=AX.X, op=ALU.max)
+
+        for c in spans:
+            nc.scalar.activation(sq_im[:, c], acc_im[:, c], ACT.Square)
+        l_add(spans[0])
+        f_max(last - 1)
+        l_mul(spans[0])
+        l_add(spans[1])
+        l_add(spans[2])
+        l_mul(spans[1])
+        l_mul(spans[2])
+        nc.vector.tensor_reduce(out=st[:, B : B + 1], in_=st[:, 0:384], axis=AX.X, op=ALU.max)
+        nc.vector.tensor_reduce(out=peaks[:, last : last + 1], in_=st[:, 384 : B + 1], axis=AX.X, op=ALU.max)
         nc.sync.dma_start(out=po, in_=peaks[:])

@@ -18,8 +18,8 @@ P = 128
 T, K, J, B, N = 1024, 2048, 512, 512, 1024
 NT = T // P
 FLOPS = 2 * T * N * (K + J)
-PERM_ON_SCALAR = [(5, 1), (6, 1), (7, 1)]
-V_SPLIT = 320
+PERM_ON_SCALAR = []
+V_SPLIT = (256, 512)
 
 
 def tile_beamformer_detection_statistics_s1_kernel(
@@ -35,11 +35,10 @@ def tile_beamformer_detection_statistics_s1_kernel(
         keep = ctx.enter_context(tc.tile_pool(name="keep", bufs=1))
         work = ctx.enter_context(tc.tile_pool(name="work", bufs=4))
         epi = ctx.enter_context(tc.tile_pool(name="epi", bufs=4))
-        turn = ctx.enter_context(tc.psum_pool(name="turn", bufs=4))
-        accs = ctx.enter_context(tc.psum_pool(name="accs", bufs=2))
+        psum = ctx.enter_context(tc.psum_pool(name="psum", bufs=1))
 
-        wsc = keep.tile([P, 4 * N], U8, align_bytes=64, name="wsc")
-        nc.vector.memset(wsc[:].bitcast(I32), 0)
+        wsc = keep.tile([P, 4, N], U8, align_bytes=64, name="wsc")
+        nc.vector.memset(wsc[:].rearrange("p g n -> p (g n)").bitcast(I32), 0)
         zeros = keep.tile([P, B], BF16, align_bytes=64, name="zeros")
         nc.vector.memset(zeros[:], 0.0)
         ones = keep.tile([P, P], BF16, align_bytes=64, name="ones")
@@ -51,77 +50,89 @@ def tile_beamformer_detection_statistics_s1_kernel(
         ident = keep.tile([P, P], F32, align_bytes=64, name="ident")
         make_identity(nc, ident[:])
         ctx.enter_context(tc.manual_schedule())
+        nc.scalar.activation(warm[:, 1:2], warm[:, 0:1], ACT.Square)
 
-        raws = {}
+        raws, w_tiles, v_raws = {}, {}, []
 
-        def load_main(i, split):
-            if split:
-                for h in (0, 1):
-                    r = keep.tile([P, 1024], BF16, align_bytes=64, name="raw%d_%d" % (i, h))
-                    nc.sync.dma_start(out=r[:], in_=xm[:, i, 1024 * h : 1024 * (h + 1)])
-                    raws[(i, h)] = r[:]
-            else:
-                r = keep.tile([P, 2048], BF16, align_bytes=64, name="raw%d" % i)
-                nc.sync.dma_start(out=r[:], in_=xm[:, i, :])
-                for h in (0, 1):
-                    raws[(i, h)] = r[:, 1024 * h : 1024 * (h + 1)]
+        def load_main(i, split=False):
+            r = [keep.tile([P, 1024], BF16, align_bytes=64, name="raw%d_%d" % (i, h)) for h in (0, 1)] if split else [keep.tile([P, 2048], BF16, align_bytes=64, name="raw%d" % i)]
+            for h, t in enumerate(r):
+                w = K // len(r)
+                nc.sync.dma_start(out=t[:], in_=xm[:, i, w * h : w * (h + 1)])
+            for h in (0, 1):
+                raws[(i, h)] = r[h][:] if split else r[0][:, 1024 * h : 1024 * (h + 1)]
 
         def load_aux(i):
             r = keep.tile([P, 2, J], BF16, align_bytes=64, name="rawa%d" % i)
             nc.sync.dma_start(out=r[:], in_=xa[:, i : i + 2, :])
             raws[(i, 2)] = r[:].rearrange("p s k -> p (s k)")
 
-        load_main(0, True)
-        w_tiles = []
-
-        def load_w(c):
-            wt = keep.tile([P, 2, 2 * N], U8, align_bytes=64, name="w%d" % c)
-            nc.sync.dma_start(out=wt[:].bitcast(I32), in_=w_words[2 * c : 2 * c + 2].bitcast(I32).rearrange("g p b -> p g b"))
-            w_tiles.extend([wt[:, 0, :], wt[:, 1, :]])
+        def load_w(lo, hi):
+            t = keep.tile([P, hi - lo, 2 * N], U8, align_bytes=64, name="w%d" % lo)
+            nc.sync.dma_start(out=t[:].bitcast(I32), in_=w_words[lo:hi].bitcast(I32).rearrange("g p b -> p g b"))
+            for g in range(lo, hi):
+                w_tiles[g] = t[:, g - lo, :]
 
         ws_i32 = w_scales.bitcast(I32)
-        for q in range(4):
-            nc.sync.dma_start(
-                out=wsc[32 * q : 32 * q + 4, :].bitcast(I32).rearrange("p (g n) -> p g n", g=4),
-                in_=ws_i32[:, 4 * q : 4 * q + 4, :].rearrange("g r n -> r g n"),
-            )
-        nc.scalar.activation(warm[:, 1:2], warm[:, 0:1], ACT.Square)
-        load_main(1, False)
-        load_w(0)
-        load_w(1)
-        load_aux(0)
+
+        def load_s(lo, hi):
+            for q in range(4):
+                nc.sync.dma_start(
+                    out=wsc[32 * q : 32 * q + 4, lo:hi, :].bitcast(I32),
+                    in_=ws_i32[lo:hi, 4 * q : 4 * q + 4, :].rearrange("g r n -> r g n"),
+                )
+
         v_view = v.rearrange("(p j) n -> p j n", j=4)
-        v_raws = []
-        for h in (0, 1):
+
+        def load_v(h):
             vr = keep.tile([P, 4, 512], BF16, align_bytes=64, name="vraw%d" % h)
             nc.sync.dma_start(out=vr[:], in_=v_view[:, :, 512 * h : 512 * (h + 1)])
             v_raws.append(vr)
+
+        load_main(0, True)
+        load_main(1)
+        load_s(0, 2)
+        load_w(0, 1)
+        load_w(1, 2)
         nc.sync.dma_start(out=inv_row[0:1, :], in_=inv_noise.rearrange("(o b) -> o b", o=1))
-        for i in range(2, NT):
-            load_main(i, False)
-            if i % 2 == 1:
-                load_aux(i - 1)
+        load_main(2)
+        load_main(3)
+        load_aux(0)
+        load_aux(2)
+        load_s(2, 4)
+        load_w(2, 4)
+        load_main(4)
+        load_v(0)
+        load_v(1)
+        load_main(5)
+        load_aux(4)
+        load_main(6)
+        load_main(7)
+        load_aux(6)
 
         xps, xts, grps, codes = {}, {}, {}, {}
 
+        def bank(b):
+            return psum.tile([P, 512], F32, name="bank%d" % b)
+
         def perm(u):
-            xp = work.tile([P, 2, 2, P], F32, align_bytes=64, name="xp", bufs=6)
+            xp = work.tile([P, 2, 2, P], F32, align_bytes=64, name="xp", bufs=10)
             copy = nc.scalar.copy if u in PERM_ON_SCALAR else nc.vector.tensor_copy
             copy(out=xp[:], in_=raws[u].bitcast(F32).rearrange("p (s a u) -> p s u a", s=2, u=2))
             xps[u] = xp
 
-        def trans(u):
-            xt = turn.tile([P, 2, 2, P], F32, name="xt")
-            for s in (0, 1):
-                for w in (0, 1):
-                    nc.tensor.transpose(xt[:, s, w, :], xps[u][:, s, w, :], ident[:])
-            xts[u] = xt
+        def trans(u, b):
+            t = bank(b)
+            xts[u] = t
+            for q in range(4):
+                nc.tensor.transpose(t[:, P * q : P * (q + 1)], xps[u][:, q // 2, q % 2, :], ident[:])
 
-        def drain(u):
-            grp = work.tile([P, 1024], BF16, align_bytes=64, name="grp", bufs=4)
-            nc.scalar.copy(
+        def drain(u, on_vector=False):
+            grp = work.tile([P, 1024], BF16, align_bytes=64, name="grp", bufs=10)
+            copy = nc.vector.tensor_copy if on_vector else nc.scalar.copy
+            copy(
                 out=grp[:].bitcast(F32).rearrange("p (s r u) -> p s r u", s=2, u=2),
-                in_=xts[u][:].rearrange("p s u r -> p s r u"),
+                in_=xts[u][:].rearrange("p (s u r) -> p s r u", s=2, u=2),
             )
             grps[u] = grp
 
@@ -134,206 +145,209 @@ def tile_beamformer_detection_statistics_s1_kernel(
         v_grps, v_codes = [], []
         for h in (0, 1):
             v_grps.append(keep.tile([P, 512, 4], BF16, align_bytes=64, name="vgrp%d" % h))
-            v_codes.append(
-                (
-                    keep.tile([P, 512], U32, align_bytes=64, name="vcode%d" % h),
-                    keep.tile([P, 512], U8, align_bytes=64, name="vscale%d" % h),
-                )
-            )
+            v_codes.append((keep.tile([P, 512], U32, align_bytes=64, name="vcode%d" % h), keep.tile([P, 512], U8, align_bytes=64, name="vscale%d" % h)))
 
-        def v_inter(h):
+        def v_inter(h, lo, hi, scalar=False):
             src = v_raws[h][:].rearrange("p t n -> p n t")
-            nc.vector.tensor_copy(out=v_grps[h][:, 0:V_SPLIT, :], in_=src[:, 0:V_SPLIT, :])
-            nc.scalar.copy(out=v_grps[h][:, V_SPLIT:512, :], in_=src[:, V_SPLIT:512, :])
+            copy = nc.scalar.copy if scalar else nc.vector.tensor_copy
+            copy(out=v_grps[h][:, lo:hi, :], in_=src[:, lo:hi, :])
 
         def v_quant(h):
             c, sc = v_codes[h]
-            nc.vector.quantize_mx(
-                out=c[:].bitcast(FP8X4), scales=sc[:], in_=v_grps[h][:].rearrange("p n t -> p (n t)")
-            )
+            nc.vector.quantize_mx(out=c[:].bitcast(FP8X4), scales=sc[:], in_=v_grps[h][:].rearrange("p n t -> p (n t)"))
 
         acc = {}
 
-        def mm_main(i, halves=(0, 1)):
-            if 0 in halves:
-                re = accs.tile([P, 512], F32, name="acc_re")
-                im = accs.tile([P, 512], F32, name="acc_im")
-                acc[i] = (re, im)
-            for g in range(4):
-                c, sc = codes[(i, g // 2)]
-                cols = slice(P * (g % 2), P * (g % 2) + P)
-                for h in halves:
-                    nc.tensor.matmul_mx(
-                        out=acc[i][h][:],
-                        lhsT=c[:, cols].bitcast(FP8X4),
-                        lhsT_scale=sc[:, cols],
-                        rhs=w_tiles[g][:, 1024 * h : 1024 * (h + 1)].bitcast(FP4X4),
-                        rhs_scale=wsc[:, N * g + 512 * h : N * g + 512 * (h + 1)],
-                        start=(g == 0),
-                        stop=False,
-                    )
+        def mm(i, h, groups):
+            for g in groups:
+                c, sc = codes[(i, g // 2)] if g < 4 else codes[(i - i % 2, 2)]
+                s = g % 2 if g < 4 else i % 2
+                cols = slice(P * s, P * (s + 1))
+                if g < 4:
+                    rhs, rsc = w_tiles[g][:, 1024 * h : 1024 * (h + 1)].bitcast(FP4X4), wsc[:, g, 512 * h : 512 * (h + 1)]
+                else:
+                    rhs, rsc = v_codes[h][0][:].bitcast(FP8X4), v_codes[h][1][:]
+                nc.tensor.matmul_mx(out=acc[i][h][:], lhsT=c[:, cols].bitcast(FP8X4), lhsT_scale=sc[:, cols], rhs=rhs, rhs_scale=rsc, start=(g == 0), stop=(g == 4))
 
-        def mm_aux(i, halves=(0, 1)):
-            c, sc = codes[(i - i % 2, 2)]
-            cols = slice(P * (i % 2), P * (i % 2) + P)
-            for h in halves:
-                vc, vs = v_codes[h]
-                nc.tensor.matmul_mx(
-                    out=acc[i][h][:],
-                    lhsT=c[:, cols].bitcast(FP8X4),
-                    lhsT_scale=sc[:, cols],
-                    rhs=vc[:].bitcast(FP8X4),
-                    rhs_scale=vs[:],
-                    start=False,
-                    stop=True,
-                )
+        def mm_both(i, groups):
+            for g in groups:
+                mm(i, 0, [g])
+                mm(i, 1, [g])
 
         sqs, sums, stats = {}, {}, {}
         peaks = keep.tile([P, NT], F32, align_bytes=64, name="peaks")
         inv = keep.tile([P, B], F32, align_bytes=64, name="inv")
+        ALL = [slice(0, B)]
+        HALVES = [slice(0, 256), slice(256, B)]
 
-        def square(i, h):
+        def square(i, h, parts=ALL):
             sq = epi.tile([P, B], F32, name="sq%d" % h)
-            nc.scalar.activation(sq[:], acc[i][h][:], ACT.Square)
+            for c in parts:
+                nc.scalar.activation(sq[:, c], acc[i][h][:, c], ACT.Square)
             sqs[(i, h)] = sq
 
-        def f_add(i, c=slice(0, B)):
+        def f_add(i, c):
             if i not in sums:
-                sums[i] = epi.tile([P, B], F32, name="sm")
+                sm = epi.tile([P, B], F32, name="sm")
+                sums[i] = sm
             nc.vector.tensor_tensor(out=sums[i][:, c], in0=sqs[(i, 0)][:, c], in1=sqs[(i, 1)][:, c], op=ALU.add)
 
-        def f_mul(i, c=slice(0, B)):
+        def f_mul(i, c):
             if i not in stats:
-                stats[i] = epi.tile([P, B], F32, name="st")
+                st = epi.tile([P, B], F32, name="st")
+                stats[i] = st
             nc.vector.tensor_tensor(out=stats[i][:, c], in0=sums[i][:, c], in1=inv[:, c], op=ALU.mult)
-            if c.stop == B:
+            if i == NT - 1:
+                nc.sync.dma_start(out=so[:, i, c], in_=stats[i][:, c])
+            elif c.stop == B:
                 nc.sync.dma_start(out=so[:, i, :], in_=stats[i][:])
 
         def f_max(i):
             nc.vector.tensor_reduce(out=peaks[:, i : i + 1], in_=stats[i][:], axis=AX.X, op=ALU.max)
 
-        def dummies(n):
-            ps = turn.tile([P, 2, 2, P], F32, name="xt")
+        def dummies(n, b):
+            ps = bank(b)
             for k in range(n):
-                nc.tensor.matmul(ps[:].rearrange("p s u r -> p (s u r)"), lhsT=ones[:], rhs=zeros[:], start=True, stop=True)
+                nc.tensor.matmul(ps[:], lhsT=ones[:], rhs=zeros[:], start=True, stop=True)
 
-        dummies(4)
-        head = [(0, 0), (0, 1), (1, 0), (1, 1)]
-        for u in head:
-            perm(u)
-        for u in head:
-            trans(u)
-            drain(u)
-            quant(u)
-            if u[1] == 1:
-                dummies(1)
-        mm_main(0)
-        perm((0, 2))
-        trans((0, 2))
-        mm_main(1)
-        v_inter(0)
-        drain((0, 2))
-        v_inter(1)
-        for u in [(2, 0), (2, 1)]:
-            perm(u)
-        v_quant(0)
-        quant((0, 2))
-        v_quant(1)
-        inv_ps = turn.tile([P, 2, 2, P], F32, name="xt")
-        nc.tensor.matmul(inv_ps[:].rearrange("p s u r -> p (s u r)"), lhsT=ones[:], rhs=inv_row[:], start=True, stop=True)
-        nc.scalar.copy(out=inv[:], in_=inv_ps[:].rearrange("p s u r -> p (s u r)"))
-        for u in [(2, 0), (2, 1)]:
-            trans(u)
-            drain(u)
-        mm_aux(0)
-        mm_aux(1)
-        square(0, 0)
-        square(0, 1)
-        perm((3, 0))
-        perm((3, 1))
-        quant((2, 0))
-        perm((2, 2))
-        quant((2, 1))
-
-        turns = {
-            2: [(3, 0), (3, 1), (2, 2)],
-            3: [(4, 0), (4, 1), (4, 2)],
-            4: [(5, 0), (5, 1)],
-            5: [(6, 0), (6, 1), (6, 2)],
-            6: [(7, 0), (7, 1)],
-        }
-        finishes = {2: [0], 3: [1], 4: [2, 3], 5: [4], 6: [5], 7: [6]}
-        for i in range(2, NT):
-            turned = turns.get(i, [])
-            laid = turns.get(i + 1, [])
-            for u in turned:
-                trans(u)
-            if i > 2:
-                square(i - 1, 0)
-                square(i - 1, 1)
-            for u in turned:
-                drain(u)
-            if i == 2:
-                square(1, 0)
-                square(1, 1)
-            a = [lambda u=u: perm(u) for u in laid[:1]] + [lambda u=u: quant(u) for u in turned] + [lambda u=u: perm(u) for u in laid[1:]]
-            if i < 6:
-                b = [lambda f=f, j=j: f(j) for f in (f_add, f_mul, f_max) for j in finishes[i]]
-            else:
-                b = [lambda f=f, c=c: f(i - 1, c) for f in (f_add, f_mul) for c in (slice(0, 256), slice(256, B))]
-                if i == 6:
-                    b.append(lambda: f_max(i - 1))
+        def weave(a, b):
             for k in range(max(len(a), len(b))):
-                if k < len(a):
-                    a[k]()
-                if k < len(b):
-                    b[k]()
-            if i < NT - 1:
-                mm_main(i)
-                mm_aux(i)
+                for s in (a, b):
+                    if k < len(s):
+                        s[k]()
 
+        dummies(4, 7)
+        first = ((0, 0), (0, 1), (1, 0), (1, 1))
+        second = ((2, 0), (2, 1), (3, 0), (3, 1), (0, 2), (2, 2))
+        for u in first[:2]:
+            perm(u)
+            trans(u, u[1])
+            drain(u)
+        for u in first[2:]:
+            perm(u)
+            trans(u, 2 + u[1])
+            drain(u)
+        for u in first:
+            quant(u)
+        acc[0] = (bank(4), bank(5))
+        acc[1] = (bank(6), bank(7))
+        for g in (0, 1):
+            mm_both(0, [g])
+            mm_both(1, [g])
+        inv_ps = bank(1)
+        nc.tensor.matmul(inv_ps[:], lhsT=ones[:], rhs=inv_row[:], start=True, stop=True)
+        nc.scalar.copy(out=inv[:], in_=inv_ps[:])
+        for u in second:
+            perm(u)
+        for k, u in enumerate(second):
+            trans(u, k % 4)
+            drain(u)
+            if k >= 3:
+                quant(second[k - 3])
+        for u in second[3:]:
+            quant(u)
+        acc[2] = (bank(2), bank(3))
+        mm_both(2, [0, 1])
+        for i in (0, 1, 2):
+            mm_both(i, [2])
+        for h in (0, 1):
+            perm((4, h))
+            trans((4, h), 1 - h)
+        for i in (0, 1, 2):
+            mm_both(i, [3])
+        v_inter(0, 0, V_SPLIT[0])
+        if V_SPLIT[0] < 512:
+            v_inter(0, V_SPLIT[0], 512, True)
+        for h in (0, 1):
+            drain((4, h))
+        v_quant(0)
+        v_inter(1, 0, V_SPLIT[1])
+        if V_SPLIT[1] < 512:
+            v_inter(1, V_SPLIT[1], 512, True)
+        for i in (0, 1, 2):
+            mm(i, 0, [4])
+            square(i, 0)
+        quant((4, 0))
+        quant((4, 1))
+        v_quant(1)
+        acc[3] = (bank(1), bank(0))
+        mm_both(3, range(4))
+        for i in (0, 1, 2):
+            mm(i, 1, [4])
+            square(i, 1)
+        third = ((4, 2), (5, 0), (5, 1), (6, 0))
+        fourth = ((6, 1), (6, 2), (7, 0), (7, 1))
+        for u, b in zip(third, (4, 6, 2, 5)):
+            perm(u)
+            trans(u, b)
+        mm_both(3, [4])
+        A = ALL[0]
+        for u in fourth:
+            perm(u)
+        f_add(0, A)
+        for u in third[:2]:
+            drain(u)
+        f_add(1, A)
+        f_mul(0, A)
+        for u in third[2:]:
+            drain(u)
+        square(3, 0)
+        square(3, 1)
+        quant(third[0])
+        f_mul(1, A)
+        quant(third[1])
+        f_max(0)
+        quant(third[2])
+        f_add(2, A)
+        quant(third[3])
+        acc[4] = (bank(7), bank(3))
+        mm_both(4, range(5))
+        for u, b in zip(fourth, (4, 6, 2, 5)):
+            trans(u, b)
+        acc[5] = (bank(0), bank(1))
+        mm_both(5, range(5))
+        f_mul(2, A)
+        f_max(1)
+        for u in fourth[:2]:
+            drain(u)
+        square(4, 0)
+        square(4, 1)
+        for u in fourth[2:]:
+            drain(u)
+        f_add(3, A)
+        quant(fourth[0])
+        f_max(2)
+        quant(fourth[1])
+        f_mul(3, A)
+        quant(fourth[2])
+        f_add(4, A)
+        quant(fourth[3])
+        f_max(3)
+        f_mul(4, A)
+        square(5, 0)
+        square(5, 1)
+        acc[6] = (bank(2), bank(5))
+        mm_both(6, range(5))
+        f_max(4)
+        for f in (f_add, f_mul):
+            for c in HALVES:
+                f(5, c)
+        acc[7] = (bank(4), bank(6))
+        mm(7, 0, range(5))
+        mm(7, 1, range(5))
+        square(6, 0)
+        square(6, 1)
+        f_max(5)
+        for f in (f_add, f_mul):
+            for c in HALVES:
+                f(6, c)
         last = NT - 1
-        mm_main(last, (0,))
-        mm_aux(last, (0,))
         square(last, 0)
-        pieces = [slice(P * q, P * (q + 1)) for q in range(4)]
-        acc_im = acc[last][1]
-        for n in pieces:
-            for g in range(5):
-                c, sc = codes[(last, g // 2)] if g < 4 else codes[(last - 1, 2)]
-                cols = slice(P * (g % 2), P * (g % 2) + P) if g < 4 else slice(P, 2 * P)
-                w = w_tiles[g][:, 1024 + 2 * n.start : 1024 + 2 * n.stop].bitcast(FP4X4) if g < 4 else v_codes[1][0][:, n].bitcast(FP8X4)
-                ws = wsc[:, N * g + 512 + n.start : N * g + 512 + n.stop] if g < 4 else v_codes[1][1][:, n]
-                nc.tensor.matmul_mx(
-                    out=acc_im[:, n],
-                    lhsT=c[:, cols].bitcast(FP8X4),
-                    lhsT_scale=sc[:, cols],
-                    rhs=w,
-                    rhs_scale=ws,
-                    start=(g == 0),
-                    stop=(g == 4),
-                )
-        sq_im = epi.tile([P, B], F32, name="sq1")
-        sm = epi.tile([P, B], F32, name="sm")
-        st = epi.tile([P, B + 1], F32, name="stl", bufs=1)
-        spans = [slice(0, 256), slice(256, 384), slice(384, 512)]
-
-        def l_add(c):
-            nc.vector.tensor_tensor(out=sm[:, c], in0=sqs[(last, 0)][:, c], in1=sq_im[:, c], op=ALU.add)
-
-        def l_mul(c):
-            nc.vector.tensor_tensor(out=st[:, c], in0=sm[:, c], in1=inv[:, c], op=ALU.mult)
-            nc.sync.dma_start(out=so[:, last, c], in_=st[:, c])
-
-        for c in spans:
-            nc.scalar.activation(sq_im[:, c], acc_im[:, c], ACT.Square)
-        l_add(spans[0])
+        square(last, 1, HALVES)
+        f_add(last, HALVES[0])
+        f_add(last, HALVES[1])
         f_max(last - 1)
-        l_mul(spans[0])
-        l_add(spans[1])
-        l_add(spans[2])
-        l_mul(spans[1])
-        l_mul(spans[2])
-        nc.vector.tensor_reduce(out=st[:, B : B + 1], in_=st[:, 0:384], axis=AX.X, op=ALU.max)
-        nc.vector.tensor_reduce(out=peaks[:, last : last + 1], in_=st[:, 384 : B + 1], axis=AX.X, op=ALU.max)
+        f_mul(last, HALVES[0])
+        f_mul(last, HALVES[1])
+        f_max(last)
         nc.sync.dma_start(out=po, in_=peaks[:])

@@ -8,346 +8,365 @@ BF16 = mybir.dt.bfloat16
 I32 = mybir.dt.int32
 U32 = mybir.dt.uint32
 U8 = mybir.dt.uint8
-FP8X4 = mybir.dt.float8_e4m3fn_x4
-FP4X4 = mybir.dt.float4_e2m1fn_x4
+E4M3X4 = mybir.dt.float8_e4m3fn_x4
+E2M1X4 = mybir.dt.float4_e2m1fn_x4
 ALU = mybir.AluOpType
 ACT = mybir.ActivationFunctionType
-AX = mybir.AxisListType
 
 P = 128
-T, K, J, B, N = 1024, 2048, 512, 512, 1024
-NT = T // P
-FLOPS = 2 * T * N * (K + J)
-PERM_ON_SCALAR = []
-V_SPLIT = (256, 512)
+SNAPSHOTS, MAIN, AUX, BEAMS, COLUMNS = 1024, 2048, 512, 512, 1024
+TILES = SNAPSHOTS // P
+MAIN_PASSES = MAIN // 512
+AUX_PASS = MAIN_PASSES
+CHUNK = 1024
+FLOPS = 2 * SNAPSHOTS * COLUMNS * (MAIN + AUX)
+
+TURNED_AS_LOADED = (0, 1)
+LAID_OUT_ON_SCALAR = (7, 1)
+V_SPLIT = 192
+
+WHOLE = slice(0, BEAMS)
+PIECES = (slice(0, BEAMS // 2), slice(BEAMS // 2, BEAMS))
 
 
 def tile_beamformer_detection_statistics_s1_kernel(
     tc, x_main, x_aux, w_words, w_scales, v, inv_noise, stat_out, peak_out
 ):
     nc = tc.nc
-    xm = x_main.rearrange("(p i) k -> p i k", i=NT)
-    xa = x_aux.rearrange("(p i) k -> p i k", i=NT)
-    so = stat_out.rearrange("(p i) b -> p i b", i=NT)
-    po = peak_out.rearrange("(p i) -> p i", i=NT)
+    main_rows = x_main.rearrange("(p i) k -> p i k", i=TILES)
+    aux_rows = x_aux.rearrange("(p i) k -> p i k", i=TILES)
+    stat_rows = stat_out.rearrange("(p i) b -> p i b", i=TILES)
+    peak_rows = peak_out.rearrange("(p i) -> p i", i=TILES)
+    v_rows = v.rearrange("(p t) n -> p t n", t=4)
+    scale_words = w_scales.bitcast(I32)
 
     with ExitStack() as ctx:
         keep = ctx.enter_context(tc.tile_pool(name="keep", bufs=1))
-        work = ctx.enter_context(tc.tile_pool(name="work", bufs=4))
-        epi = ctx.enter_context(tc.tile_pool(name="epi", bufs=4))
+        stage = ctx.enter_context(tc.tile_pool(name="stage", bufs=10))
+        finish = ctx.enter_context(tc.tile_pool(name="finish", bufs=4))
         psum = ctx.enter_context(tc.psum_pool(name="psum", bufs=1))
 
-        wsc = keep.tile([P, 4, N], U8, align_bytes=64, name="wsc")
-        nc.vector.memset(wsc[:].rearrange("p g n -> p (g n)").bitcast(I32), 0)
-        zeros = keep.tile([P, B], BF16, align_bytes=64, name="zeros")
+        w_scale_tile = keep.tile([P, MAIN_PASSES, COLUMNS], U8, align_bytes=64, name="w_scale_tile")
+        nc.vector.memset(w_scale_tile[:].rearrange("p g n -> p (g n)").bitcast(I32), 0)
+        zeros = keep.tile([P, BEAMS], BF16, align_bytes=64, name="zeros")
         nc.vector.memset(zeros[:], 0.0)
         ones = keep.tile([P, P], BF16, align_bytes=64, name="ones")
         nc.vector.memset(ones[:], 1.0)
-        warm = keep.tile([P, 2], F32, name="warm")
-        nc.vector.memset(warm[:], 1.0)
-        inv_row = keep.tile([P, B], BF16, align_bytes=64, name="inv_row")
-        nc.vector.memset(inv_row[:], 0.0)
-        ident = keep.tile([P, P], F32, align_bytes=64, name="ident")
-        make_identity(nc, ident[:])
+        table = keep.tile([P, 2], F32, name="table")
+        nc.vector.memset(table[:], 1.0)
+        noise_row = keep.tile([P, BEAMS], BF16, align_bytes=64, name="noise_row")
+        nc.vector.memset(noise_row[:], 0.0)
+        identity = keep.tile([P, P], F32, align_bytes=64, name="identity")
+        make_identity(nc, identity[:])
+
         ctx.enter_context(tc.manual_schedule())
-        nc.scalar.activation(warm[:, 1:2], warm[:, 0:1], ACT.Square)
 
-        raws, w_tiles, v_raws = {}, {}, []
+        nc.scalar.activation(table[:, 1:2], table[:, 0:1], ACT.Square)
 
-        def load_main(i, split=False):
-            r = [keep.tile([P, 1024], BF16, align_bytes=64, name="raw%d_%d" % (i, h)) for h in (0, 1)] if split else [keep.tile([P, 2048], BF16, align_bytes=64, name="raw%d" % i)]
-            for h, t in enumerate(r):
-                w = K // len(r)
-                nc.sync.dma_start(out=t[:], in_=xm[:, i, w * h : w * (h + 1)])
-            for h in (0, 1):
-                raws[(i, h)] = r[h][:] if split else r[0][:, 1024 * h : 1024 * (h + 1)]
+        raw = {}
+
+        def load_main(i, pieces=1):
+            width = MAIN // pieces
+            for k in range(pieces):
+                t = keep.tile([P, width], BF16, align_bytes=64, name="main%d_%d" % (i, k))
+                nc.sync.dma_start(out=t[:], in_=main_rows[:, i, width * k : width * (k + 1)])
+                for c in range(width // CHUNK):
+                    raw[(i, k + c)] = t[:, CHUNK * c : CHUNK * (c + 1)]
 
         def load_aux(i):
-            r = keep.tile([P, 2, J], BF16, align_bytes=64, name="rawa%d" % i)
-            nc.sync.dma_start(out=r[:], in_=xa[:, i : i + 2, :])
-            raws[(i, 2)] = r[:].rearrange("p s k -> p (s k)")
+            t = keep.tile([P, 2, AUX], BF16, align_bytes=64, name="aux%d" % i)
+            nc.sync.dma_start(out=t[:], in_=aux_rows[:, i : i + 2, :])
+            raw[(i, 2)] = t[:].rearrange("p s k -> p (s k)")
 
-        def load_w(lo, hi):
-            t = keep.tile([P, hi - lo, 2 * N], U8, align_bytes=64, name="w%d" % lo)
-            nc.sync.dma_start(out=t[:].bitcast(I32), in_=w_words[lo:hi].bitcast(I32).rearrange("g p b -> p g b"))
-            for g in range(lo, hi):
-                w_tiles[g] = t[:, g - lo, :]
+        w_codes = {}
 
-        ws_i32 = w_scales.bitcast(I32)
+        def load_codes(first, count):
+            t = keep.tile([P, count, 2 * COLUMNS], U8, align_bytes=64, name="codes%d" % first)
+            source = w_words[first : first + count].bitcast(I32)
+            nc.sync.dma_start(out=t[:].bitcast(I32), in_=source.rearrange("g p b -> p g b"))
+            for k in range(count):
+                w_codes[first + k] = t[:, k, :]
 
-        def load_s(lo, hi):
+        def load_scales(first, count):
             for q in range(4):
                 nc.sync.dma_start(
-                    out=wsc[32 * q : 32 * q + 4, lo:hi, :].bitcast(I32),
-                    in_=ws_i32[lo:hi, 4 * q : 4 * q + 4, :].rearrange("g r n -> r g n"),
+                    out=w_scale_tile[32 * q : 32 * q + 4, first : first + count, :].bitcast(I32),
+                    in_=scale_words[first : first + count, 4 * q : 4 * q + 4, :].rearrange("g r n -> r g n"),
                 )
 
-        v_view = v.rearrange("(p j) n -> p j n", j=4)
+        v_raw = []
 
-        def load_v(h):
-            vr = keep.tile([P, 4, 512], BF16, align_bytes=64, name="vraw%d" % h)
-            nc.sync.dma_start(out=vr[:], in_=v_view[:, :, 512 * h : 512 * (h + 1)])
-            v_raws.append(vr)
+        def load_v(half):
+            t = keep.tile([P, 4, 512], BF16, align_bytes=64, name="v%d" % half)
+            nc.sync.dma_start(out=t[:], in_=v_rows[:, :, 512 * half : 512 * (half + 1)])
+            v_raw.append(t)
 
-        load_main(0, True)
+        load_main(0, pieces=2)
         load_main(1)
-        load_s(0, 2)
-        load_w(0, 1)
-        load_w(1, 2)
-        nc.sync.dma_start(out=inv_row[0:1, :], in_=inv_noise.rearrange("(o b) -> o b", o=1))
+        load_scales(0, 2)
+        load_codes(0, 1)
+        load_codes(1, 1)
+        nc.sync.dma_start(out=noise_row[0:1, :], in_=inv_noise.rearrange("(o b) -> o b", o=1))
         load_main(2)
         load_main(3)
+        load_scales(2, 2)
+        load_codes(2, 2)
         load_aux(0)
         load_aux(2)
-        load_s(2, 4)
-        load_w(2, 4)
-        load_main(4)
         load_v(0)
         load_v(1)
-        load_main(5)
+        load_main(4)
         load_aux(4)
+        load_main(5)
         load_main(6)
-        load_main(7)
         load_aux(6)
+        load_main(7)
 
-        xps, xts, grps, codes = {}, {}, {}, {}
+        laid, turned, collected, quantized = {}, {}, {}, {}
 
         def bank(b):
             return psum.tile([P, 512], F32, name="bank%d" % b)
 
-        def perm(u):
-            xp = work.tile([P, 2, 2, P], F32, align_bytes=64, name="xp", bufs=10)
-            copy = nc.scalar.copy if u in PERM_ON_SCALAR else nc.vector.tensor_copy
-            copy(out=xp[:], in_=raws[u].bitcast(F32).rearrange("p (s a u) -> p s u a", s=2, u=2))
-            xps[u] = xp
+        def lay_out(chunk):
+            t = stage.tile([P, 2, 2, P], F32, align_bytes=64, name="laid_out")
+            copy = nc.scalar.copy if chunk == LAID_OUT_ON_SCALAR else nc.vector.tensor_copy
+            copy(out=t[:], in_=raw[chunk].bitcast(F32).rearrange("p (s a e) -> p s e a", s=2, e=2))
+            laid[chunk] = t
 
-        def trans(u, b):
+        def turn(chunk, b):
             t = bank(b)
-            xts[u] = t
-            for q in range(4):
-                nc.tensor.transpose(t[:, P * q : P * (q + 1)], xps[u][:, q // 2, q % 2, :], ident[:])
+            as_loaded = chunk[0] in TURNED_AS_LOADED and chunk[1] < 2
+            for s in (0, 1):
+                for e in (0, 1):
+                    if as_loaded:
+                        source = raw[chunk].bitcast(F32)[:, 256 * s + e : 256 * (s + 1) : 2]
+                    else:
+                        source = laid[chunk][:, s, e, :]
+                    k = 2 * s + e
+                    nc.tensor.transpose(t[:, P * k : P * (k + 1)], source, identity[:])
+            turned[chunk] = t
 
-        def drain(u, on_vector=False):
-            grp = work.tile([P, 1024], BF16, align_bytes=64, name="grp", bufs=10)
-            copy = nc.vector.tensor_copy if on_vector else nc.scalar.copy
-            copy(
-                out=grp[:].bitcast(F32).rearrange("p (s r u) -> p s r u", s=2, u=2),
-                in_=xts[u][:].rearrange("p (s u r) -> p s r u", s=2, u=2),
+        def collect(chunk):
+            t = stage.tile([P, CHUNK], BF16, align_bytes=64, name="grouped")
+            nc.scalar.copy(
+                out=t[:].bitcast(F32).rearrange("p (s r e) -> p s r e", s=2, e=2),
+                in_=turned[chunk][:].rearrange("p (s e r) -> p s r e", s=2, e=2),
             )
-            grps[u] = grp
+            collected[chunk] = t
 
-        def quant(u):
-            c = keep.tile([P, 256], U32, align_bytes=64, name="code%d_%d" % u)
-            sc = keep.tile([P, 256], U8, align_bytes=64, name="scale%d_%d" % u)
-            nc.vector.quantize_mx(out=c[:].bitcast(FP8X4), scales=sc[:], in_=grps[u][:])
-            codes[u] = (c, sc)
+        def quantize(chunk):
+            codes = keep.tile([P, 2 * P], U32, align_bytes=64, name="x_codes%d_%d" % chunk)
+            scales = keep.tile([P, 2 * P], U8, align_bytes=64, name="x_scales%d_%d" % chunk)
+            nc.vector.quantize_mx(out=codes[:].bitcast(E4M3X4), scales=scales[:], in_=collected[chunk][:])
+            quantized[chunk] = (codes, scales)
 
-        v_grps, v_codes = [], []
-        for h in (0, 1):
-            v_grps.append(keep.tile([P, 512, 4], BF16, align_bytes=64, name="vgrp%d" % h))
-            v_codes.append((keep.tile([P, 512], U32, align_bytes=64, name="vcode%d" % h), keep.tile([P, 512], U8, align_bytes=64, name="vscale%d" % h)))
+        v_grouped = [keep.tile([P, 512, 4], BF16, align_bytes=64, name="v_grouped%d" % h) for h in (0, 1)]
+        v_codes = [keep.tile([P, 512], U32, align_bytes=64, name="v_codes%d" % h) for h in (0, 1)]
+        v_scales = [keep.tile([P, 512], U8, align_bytes=64, name="v_scales%d" % h) for h in (0, 1)]
 
-        def v_inter(h, lo, hi, scalar=False):
-            src = v_raws[h][:].rearrange("p t n -> p n t")
-            copy = nc.scalar.copy if scalar else nc.vector.tensor_copy
-            copy(out=v_grps[h][:, lo:hi, :], in_=src[:, lo:hi, :])
+        def interleave_v(copy, half, lo, hi):
+            copy(out=v_grouped[half][:, lo:hi, :], in_=v_raw[half][:].rearrange("p t n -> p n t")[:, lo:hi, :])
 
-        def v_quant(h):
-            c, sc = v_codes[h]
-            nc.vector.quantize_mx(out=c[:].bitcast(FP8X4), scales=sc[:], in_=v_grps[h][:].rearrange("p n t -> p (n t)"))
+        def quantize_v(half):
+            nc.vector.quantize_mx(
+                out=v_codes[half][:].bitcast(E4M3X4),
+                scales=v_scales[half][:],
+                in_=v_grouped[half][:].rearrange("p n t -> p (n t)"),
+            )
 
-        acc = {}
+        sums = {}
 
-        def mm(i, h, groups):
-            for g in groups:
-                c, sc = codes[(i, g // 2)] if g < 4 else codes[(i - i % 2, 2)]
-                s = g % 2 if g < 4 else i % 2
-                cols = slice(P * s, P * (s + 1))
-                if g < 4:
-                    rhs, rsc = w_tiles[g][:, 1024 * h : 1024 * (h + 1)].bitcast(FP4X4), wsc[:, g, 512 * h : 512 * (h + 1)]
-                else:
-                    rhs, rsc = v_codes[h][0][:].bitcast(FP8X4), v_codes[h][1][:]
-                nc.tensor.matmul_mx(out=acc[i][h][:], lhsT=c[:, cols].bitcast(FP8X4), lhsT_scale=sc[:, cols], rhs=rhs, rhs_scale=rsc, start=(g == 0), stop=(g == 4))
+        def multiply(i, half, g):
+            codes, scales = quantized[(i - i % 2, 2) if g == AUX_PASS else (i, g // 2)]
+            s = i % 2 if g == AUX_PASS else g % 2
+            rows = slice(P * s, P * (s + 1))
+            if g == AUX_PASS:
+                moving, moving_scale = v_codes[half][:].bitcast(E4M3X4), v_scales[half][:]
+            else:
+                moving = w_codes[g][:, 1024 * half : 1024 * (half + 1)].bitcast(E2M1X4)
+                moving_scale = w_scale_tile[:, g, 512 * half : 512 * (half + 1)]
+            nc.tensor.matmul_mx(
+                out=sums[i][half][:],
+                lhsT=codes[:, rows].bitcast(E4M3X4),
+                lhsT_scale=scales[:, rows],
+                rhs=moving,
+                rhs_scale=moving_scale,
+                start=(g == 0),
+                stop=(g == AUX_PASS),
+            )
 
-        def mm_both(i, groups):
-            for g in groups:
-                mm(i, 0, [g])
-                mm(i, 1, [g])
+        def multiply_both(i, passes):
+            for g in passes:
+                for half in (0, 1):
+                    multiply(i, half, g)
 
-        sqs, sums, stats = {}, {}, {}
-        peaks = keep.tile([P, NT], F32, align_bytes=64, name="peaks")
-        inv = keep.tile([P, B], F32, align_bytes=64, name="inv")
-        ALL = [slice(0, B)]
-        HALVES = [slice(0, 256), slice(256, B)]
+        squares, powers, stats = {}, {}, {}
+        noise = keep.tile([P, BEAMS], F32, align_bytes=64, name="noise")
+        peaks = keep.tile([P, TILES], F32, align_bytes=64, name="peaks")
 
-        def square(i, h, parts=ALL):
-            sq = epi.tile([P, B], F32, name="sq%d" % h)
-            for c in parts:
-                nc.scalar.activation(sq[:, c], acc[i][h][:, c], ACT.Square)
-            sqs[(i, h)] = sq
+        def square(i, half, pieces=(WHOLE,)):
+            t = finish.tile([P, BEAMS], F32, name="square%d" % half)
+            for beams in pieces:
+                nc.scalar.activation(t[:, beams], sums[i][half][:, beams], ACT.Square)
+            squares[(i, half)] = t
 
-        def f_add(i, c):
-            if i not in sums:
-                sm = epi.tile([P, B], F32, name="sm")
-                sums[i] = sm
-            nc.vector.tensor_tensor(out=sums[i][:, c], in0=sqs[(i, 0)][:, c], in1=sqs[(i, 1)][:, c], op=ALU.add)
+        def add(i, beams=WHOLE):
+            if i not in powers:
+                power = finish.tile([P, BEAMS], F32, name="power")
+                powers[i] = power
+            nc.vector.tensor_tensor(
+                out=powers[i][:, beams], in0=squares[(i, 0)][:, beams], in1=squares[(i, 1)][:, beams], op=ALU.add
+            )
 
-        def f_mul(i, c):
+        def weigh(i, beams=WHOLE):
             if i not in stats:
-                st = epi.tile([P, B], F32, name="st")
-                stats[i] = st
-            nc.vector.tensor_tensor(out=stats[i][:, c], in0=sums[i][:, c], in1=inv[:, c], op=ALU.mult)
-            if i == NT - 1:
-                nc.sync.dma_start(out=so[:, i, c], in_=stats[i][:, c])
-            elif c.stop == B:
-                nc.sync.dma_start(out=so[:, i, :], in_=stats[i][:])
+                stat = finish.tile([P, BEAMS], F32, name="stat")
+                stats[i] = stat
+            nc.vector.tensor_tensor(
+                out=stats[i][:, beams], in0=powers[i][:, beams], in1=noise[:, beams], op=ALU.mult
+            )
+            if i == TILES - 1:
+                nc.sync.dma_start(out=stat_rows[:, i, beams], in_=stats[i][:, beams])
+            elif beams.stop == BEAMS:
+                nc.sync.dma_start(out=stat_rows[:, i, :], in_=stats[i][:])
 
-        def f_max(i):
-            nc.vector.tensor_reduce(out=peaks[:, i : i + 1], in_=stats[i][:], axis=AX.X, op=ALU.max)
+        def strongest(i):
+            nc.vector.tensor_reduce(
+                out=peaks[:, i : i + 1], in_=stats[i][:], axis=mybir.AxisListType.X, op=ALU.max
+            )
 
-        def dummies(n, b):
-            ps = bank(b)
-            for k in range(n):
-                nc.tensor.matmul(ps[:], lhsT=ones[:], rhs=zeros[:], start=True, stop=True)
+        def keep_busy(count):
+            t = bank(7)
+            for k in range(count):
+                nc.tensor.matmul(t[:], lhsT=ones[:], rhs=zeros[:], start=True, stop=True)
 
-        def weave(a, b):
-            for k in range(max(len(a), len(b))):
-                for s in (a, b):
-                    if k < len(s):
-                        s[k]()
+        keep_busy(5)
+        for i in (0, 1):
+            for c in (0, 1):
+                turn((i, c), 2 * i + c)
+                collect((i, c))
+                quantize((i, c))
+            if i == 0:
+                keep_busy(2)
+        sums[0] = (bank(4), bank(5))
+        sums[1] = (bank(6), bank(7))
+        multiply_both(0, [0])
+        multiply_both(1, [0])
+        spread = bank(1)
+        nc.tensor.matmul(spread[:], lhsT=ones[:], rhs=noise_row[:], start=True, stop=True)
+        nc.scalar.copy(out=noise[:], in_=spread[:])
+        multiply_both(0, [1])
+        multiply_both(1, [1])
 
-        dummies(4, 7)
-        first = ((0, 0), (0, 1), (1, 0), (1, 1))
-        second = ((2, 0), (2, 1), (3, 0), (3, 1), (0, 2), (2, 2))
-        for u in first[:2]:
-            perm(u)
-            trans(u, u[1])
-            drain(u)
-        for u in first[2:]:
-            perm(u)
-            trans(u, 2 + u[1])
-            drain(u)
-        for u in first:
-            quant(u)
-        acc[0] = (bank(4), bank(5))
-        acc[1] = (bank(6), bank(7))
-        for g in (0, 1):
-            mm_both(0, [g])
-            mm_both(1, [g])
-        inv_ps = bank(1)
-        nc.tensor.matmul(inv_ps[:], lhsT=ones[:], rhs=inv_row[:], start=True, stop=True)
-        nc.scalar.copy(out=inv[:], in_=inv_ps[:])
-        for u in second:
-            perm(u)
-        for k, u in enumerate(second):
-            trans(u, k % 4)
-            drain(u)
-            if k >= 3:
-                quant(second[k - 3])
-        for u in second[3:]:
-            quant(u)
-        acc[2] = (bank(2), bank(3))
-        mm_both(2, [0, 1])
+        chunks = ((2, 0), (2, 1), (3, 0), (3, 1))
+        for chunk in chunks:
+            lay_out(chunk)
+        for chunk, b in zip(chunks, (2, 3, 0, 1)):
+            turn(chunk, b)
+            collect(chunk)
+        for chunk in chunks:
+            quantize(chunk)
+        sums[2] = (bank(2), bank(3))
+        multiply_both(2, [0, 1])
         for i in (0, 1, 2):
-            mm_both(i, [2])
-        for h in (0, 1):
-            perm((4, h))
-            trans((4, h), 1 - h)
+            multiply_both(i, [2])
+        for chunk, b in (((0, 2), 0), ((2, 2), 1)):
+            lay_out(chunk)
+            turn(chunk, b)
+            collect(chunk)
         for i in (0, 1, 2):
-            mm_both(i, [3])
-        v_inter(0, 0, V_SPLIT[0])
-        if V_SPLIT[0] < 512:
-            v_inter(0, V_SPLIT[0], 512, True)
-        for h in (0, 1):
-            drain((4, h))
-        v_quant(0)
-        v_inter(1, 0, V_SPLIT[1])
-        if V_SPLIT[1] < 512:
-            v_inter(1, V_SPLIT[1], 512, True)
+            multiply_both(i, [3])
+
+        interleave_v(nc.vector.tensor_copy, 0, 0, 512)
+        quantize_v(0)
+        quantize((0, 2))
+        quantize((2, 2))
+        sums[3] = (bank(0), bank(1))
+        multiply_both(3, [0, 1])
+        interleave_v(nc.vector.tensor_copy, 1, 0, V_SPLIT)
+        interleave_v(nc.scalar.copy, 1, V_SPLIT, 512)
+        quantize_v(1)
         for i in (0, 1, 2):
-            mm(i, 0, [4])
+            multiply(i, 0, AUX_PASS)
             square(i, 0)
-        quant((4, 0))
-        quant((4, 1))
-        v_quant(1)
-        acc[3] = (bank(1), bank(0))
-        mm_both(3, range(4))
         for i in (0, 1, 2):
-            mm(i, 1, [4])
-            square(i, 1)
-        third = ((4, 2), (5, 0), (5, 1), (6, 0))
-        fourth = ((6, 1), (6, 2), (7, 0), (7, 1))
-        for u, b in zip(third, (4, 6, 2, 5)):
-            perm(u)
-            trans(u, b)
-        mm_both(3, [4])
-        A = ALL[0]
-        for u in fourth:
-            perm(u)
-        f_add(0, A)
-        for u in third[:2]:
-            drain(u)
-        f_add(1, A)
-        f_mul(0, A)
-        for u in third[2:]:
-            drain(u)
+            multiply(i, 1, AUX_PASS)
+
+        for chunk in ((4, 0), (4, 1), (4, 2), (5, 0), (5, 1), (6, 0), (6, 1), (6, 2)):
+            lay_out(chunk)
+        for c, b in enumerate((4, 6, 2)):
+            turn((4, c), b)
+            square(c, 1)
+            collect((4, c))
+        multiply_both(3, [2, 3, AUX_PASS])
+        add(0)
+        quantize((4, 0))
+        add(1)
+        weigh(0)
+        quantize((4, 1))
+        add(2)
+        quantize((4, 2))
+        weigh(1)
+        strongest(0)
+
+        for chunk, b in (((5, 0), 5), ((5, 1), 7), ((6, 0), 3), ((6, 1), 4)):
+            turn(chunk, b)
+            collect(chunk)
         square(3, 0)
         square(3, 1)
-        quant(third[0])
-        f_mul(1, A)
-        quant(third[1])
-        f_max(0)
-        quant(third[2])
-        f_add(2, A)
-        quant(third[3])
-        acc[4] = (bank(7), bank(3))
-        mm_both(4, range(5))
-        for u, b in zip(fourth, (4, 6, 2, 5)):
-            trans(u, b)
-        acc[5] = (bank(0), bank(1))
-        mm_both(5, range(5))
-        f_mul(2, A)
-        f_max(1)
-        for u in fourth[:2]:
-            drain(u)
+        lay_out((7, 0))
+        lay_out((7, 1))
+        sums[4] = (bank(6), bank(2))
+        multiply_both(4, range(5))
+        quantize((5, 0))
+        weigh(2)
+        quantize((5, 1))
+        strongest(1)
+        quantize((6, 0))
+        add(3)
+        quantize((6, 1))
+        strongest(2)
+        weigh(3)
+
+        for chunk, b in (((6, 2), 5), ((7, 0), 7), ((7, 1), 3)):
+            turn(chunk, b)
+            collect(chunk)
         square(4, 0)
         square(4, 1)
-        for u in fourth[2:]:
-            drain(u)
-        f_add(3, A)
-        quant(fourth[0])
-        f_max(2)
-        quant(fourth[1])
-        f_mul(3, A)
-        quant(fourth[2])
-        f_add(4, A)
-        quant(fourth[3])
-        f_max(3)
-        f_mul(4, A)
+        sums[5] = (bank(0), bank(1))
+        multiply_both(5, range(5))
+        quantize((6, 2))
+        strongest(3)
+        quantize((7, 0))
+        add(4)
+        quantize((7, 1))
+        weigh(4)
         square(5, 0)
         square(5, 1)
-        acc[6] = (bank(2), bank(5))
-        mm_both(6, range(5))
-        f_max(4)
-        for f in (f_add, f_mul):
-            for c in HALVES:
-                f(5, c)
-        acc[7] = (bank(4), bank(6))
-        mm(7, 0, range(5))
-        mm(7, 1, range(5))
+        sums[6] = (bank(6), bank(2))
+        multiply_both(6, range(5))
+        add(5, PIECES[0])
+        strongest(4)
+        add(5, PIECES[1])
+        for beams in PIECES:
+            weigh(5, beams)
+        sums[7] = (bank(5), bank(4))
+        for half in (0, 1):
+            for g in range(5):
+                multiply(7, half, g)
         square(6, 0)
         square(6, 1)
-        f_max(5)
-        for f in (f_add, f_mul):
-            for c in HALVES:
-                f(6, c)
-        last = NT - 1
-        square(last, 0)
-        square(last, 1, HALVES)
-        f_add(last, HALVES[0])
-        f_add(last, HALVES[1])
-        f_max(last - 1)
-        f_mul(last, HALVES[0])
-        f_mul(last, HALVES[1])
-        f_max(last)
-        nc.sync.dma_start(out=po, in_=peaks[:])
+        strongest(5)
+        for beams in PIECES:
+            add(6, beams)
+        for beams in PIECES:
+            weigh(6, beams)
+        square(7, 0)
+        square(7, 1, PIECES)
+        strongest(6)
+        for beams in PIECES:
+            add(7, beams)
+        for beams in PIECES:
+            weigh(7, beams)
+        strongest(7)
+        nc.sync.dma_start(out=peak_rows, in_=peaks[:])

from contextlib import ExitStack

import concourse.mybir as mybir
from concourse.masks import make_identity

F32 = mybir.dt.float32
BF16 = mybir.dt.bfloat16
I32 = mybir.dt.int32
U32 = mybir.dt.uint32
U8 = mybir.dt.uint8
E4M3X4 = mybir.dt.float8_e4m3fn_x4
E2M1X4 = mybir.dt.float4_e2m1fn_x4
ALU = mybir.AluOpType
ACT = mybir.ActivationFunctionType

P = 128
SNAPSHOTS, MAIN, AUX, BEAMS, COLUMNS = 1024, 2048, 512, 512, 1024
TILES = SNAPSHOTS // P
MAIN_PASSES = MAIN // 512
AUX_PASS = MAIN_PASSES
CHUNK = 1024
FLOPS = 2 * SNAPSHOTS * COLUMNS * (MAIN + AUX)

TURNED_AS_LOADED = (0, 1)
LAID_OUT_ON_SCALAR = (7, 1)
V_SPLIT = 192

WHOLE = slice(0, BEAMS)
PIECES = (slice(0, BEAMS // 2), slice(BEAMS // 2, BEAMS))


def tile_beamformer_detection_statistics_s1_kernel(
    tc, x_main, x_aux, w_words, w_scales, v, inv_noise, stat_out, peak_out
):
    nc = tc.nc
    main_rows = x_main.rearrange("(p i) k -> p i k", i=TILES)
    aux_rows = x_aux.rearrange("(p i) k -> p i k", i=TILES)
    stat_rows = stat_out.rearrange("(p i) b -> p i b", i=TILES)
    peak_rows = peak_out.rearrange("(p i) -> p i", i=TILES)
    v_rows = v.rearrange("(p t) n -> p t n", t=4)
    scale_words = w_scales.bitcast(I32)

    with ExitStack() as ctx:
        keep = ctx.enter_context(tc.tile_pool(name="keep", bufs=1))
        stage = ctx.enter_context(tc.tile_pool(name="stage", bufs=10))
        finish = ctx.enter_context(tc.tile_pool(name="finish", bufs=4))
        psum = ctx.enter_context(tc.psum_pool(name="psum", bufs=1))

        w_scale_tile = keep.tile([P, MAIN_PASSES, COLUMNS], U8, align_bytes=64, name="w_scale_tile")
        nc.vector.memset(w_scale_tile[:].rearrange("p g n -> p (g n)").bitcast(I32), 0)
        zeros = keep.tile([P, BEAMS], BF16, align_bytes=64, name="zeros")
        nc.vector.memset(zeros[:], 0.0)
        ones = keep.tile([P, P], BF16, align_bytes=64, name="ones")
        nc.vector.memset(ones[:], 1.0)
        table = keep.tile([P, 2], F32, name="table")
        nc.vector.memset(table[:], 1.0)
        noise_row = keep.tile([P, BEAMS], BF16, align_bytes=64, name="noise_row")
        nc.vector.memset(noise_row[:], 0.0)
        identity = keep.tile([P, P], F32, align_bytes=64, name="identity")
        make_identity(nc, identity[:])

        ctx.enter_context(tc.manual_schedule())

        nc.scalar.activation(table[:, 1:2], table[:, 0:1], ACT.Square)

        raw = {}

        def load_main(i, pieces=1):
            width = MAIN // pieces
            for k in range(pieces):
                t = keep.tile([P, width], BF16, align_bytes=64, name="main%d_%d" % (i, k))
                nc.sync.dma_start(out=t[:], in_=main_rows[:, i, width * k : width * (k + 1)])
                for c in range(width // CHUNK):
                    raw[(i, k + c)] = t[:, CHUNK * c : CHUNK * (c + 1)]

        def load_aux(i):
            t = keep.tile([P, 2, AUX], BF16, align_bytes=64, name="aux%d" % i)
            nc.sync.dma_start(out=t[:], in_=aux_rows[:, i : i + 2, :])
            raw[(i, 2)] = t[:].rearrange("p s k -> p (s k)")

        w_codes = {}

        def load_codes(first, count):
            t = keep.tile([P, count, 2 * COLUMNS], U8, align_bytes=64, name="codes%d" % first)
            source = w_words[first : first + count].bitcast(I32)
            nc.sync.dma_start(out=t[:].bitcast(I32), in_=source.rearrange("g p b -> p g b"))
            for k in range(count):
                w_codes[first + k] = t[:, k, :]

        def load_scales(first, count):
            for q in range(4):
                nc.sync.dma_start(
                    out=w_scale_tile[32 * q : 32 * q + 4, first : first + count, :].bitcast(I32),
                    in_=scale_words[first : first + count, 4 * q : 4 * q + 4, :].rearrange("g r n -> r g n"),
                )

        v_raw = []

        def load_v(half):
            t = keep.tile([P, 4, 512], BF16, align_bytes=64, name="v%d" % half)
            nc.sync.dma_start(out=t[:], in_=v_rows[:, :, 512 * half : 512 * (half + 1)])
            v_raw.append(t)

        load_main(0, pieces=2)
        load_main(1)
        load_scales(0, 2)
        load_codes(0, 1)
        load_codes(1, 1)
        nc.sync.dma_start(out=noise_row[0:1, :], in_=inv_noise.rearrange("(o b) -> o b", o=1))
        load_main(2)
        load_main(3)
        load_scales(2, 2)
        load_codes(2, 2)
        load_aux(0)
        load_aux(2)
        load_v(0)
        load_v(1)
        load_main(4)
        load_aux(4)
        load_main(5)
        load_main(6)
        load_aux(6)
        load_main(7)

        laid, turned, collected, quantized = {}, {}, {}, {}

        def bank(b):
            return psum.tile([P, 512], F32, name="bank%d" % b)

        def lay_out(chunk):
            t = stage.tile([P, 2, 2, P], F32, align_bytes=64, name="laid_out")
            copy = nc.scalar.copy if chunk == LAID_OUT_ON_SCALAR else nc.vector.tensor_copy
            copy(out=t[:], in_=raw[chunk].bitcast(F32).rearrange("p (s a e) -> p s e a", s=2, e=2))
            laid[chunk] = t

        def turn(chunk, b):
            t = bank(b)
            as_loaded = chunk[0] in TURNED_AS_LOADED and chunk[1] < 2
            for s in (0, 1):
                for e in (0, 1):
                    if as_loaded:
                        source = raw[chunk].bitcast(F32)[:, 256 * s + e : 256 * (s + 1) : 2]
                    else:
                        source = laid[chunk][:, s, e, :]
                    k = 2 * s + e
                    nc.tensor.transpose(t[:, P * k : P * (k + 1)], source, identity[:])
            turned[chunk] = t

        def collect(chunk):
            t = stage.tile([P, CHUNK], BF16, align_bytes=64, name="grouped")
            nc.scalar.copy(
                out=t[:].bitcast(F32).rearrange("p (s r e) -> p s r e", s=2, e=2),
                in_=turned[chunk][:].rearrange("p (s e r) -> p s r e", s=2, e=2),
            )
            collected[chunk] = t

        def quantize(chunk):
            codes = keep.tile([P, 2 * P], U32, align_bytes=64, name="x_codes%d_%d" % chunk)
            scales = keep.tile([P, 2 * P], U8, align_bytes=64, name="x_scales%d_%d" % chunk)
            nc.vector.quantize_mx(out=codes[:].bitcast(E4M3X4), scales=scales[:], in_=collected[chunk][:])
            quantized[chunk] = (codes, scales)

        v_grouped = [keep.tile([P, 512, 4], BF16, align_bytes=64, name="v_grouped%d" % h) for h in (0, 1)]
        v_codes = [keep.tile([P, 512], U32, align_bytes=64, name="v_codes%d" % h) for h in (0, 1)]
        v_scales = [keep.tile([P, 512], U8, align_bytes=64, name="v_scales%d" % h) for h in (0, 1)]

        def interleave_v(copy, half, lo, hi):
            copy(out=v_grouped[half][:, lo:hi, :], in_=v_raw[half][:].rearrange("p t n -> p n t")[:, lo:hi, :])

        def quantize_v(half):
            nc.vector.quantize_mx(
                out=v_codes[half][:].bitcast(E4M3X4),
                scales=v_scales[half][:],
                in_=v_grouped[half][:].rearrange("p n t -> p (n t)"),
            )

        sums = {}

        def multiply(i, half, g):
            codes, scales = quantized[(i - i % 2, 2) if g == AUX_PASS else (i, g // 2)]
            s = i % 2 if g == AUX_PASS else g % 2
            rows = slice(P * s, P * (s + 1))
            if g == AUX_PASS:
                moving, moving_scale = v_codes[half][:].bitcast(E4M3X4), v_scales[half][:]
            else:
                moving = w_codes[g][:, 1024 * half : 1024 * (half + 1)].bitcast(E2M1X4)
                moving_scale = w_scale_tile[:, g, 512 * half : 512 * (half + 1)]
            nc.tensor.matmul_mx(
                out=sums[i][half][:],
                lhsT=codes[:, rows].bitcast(E4M3X4),
                lhsT_scale=scales[:, rows],
                rhs=moving,
                rhs_scale=moving_scale,
                start=(g == 0),
                stop=(g == AUX_PASS),
            )

        def multiply_both(i, passes):
            for g in passes:
                for half in (0, 1):
                    multiply(i, half, g)

        squares, powers, stats = {}, {}, {}
        noise = keep.tile([P, BEAMS], F32, align_bytes=64, name="noise")
        peaks = keep.tile([P, TILES], F32, align_bytes=64, name="peaks")

        def square(i, half, pieces=(WHOLE,)):
            t = finish.tile([P, BEAMS], F32, name="square%d" % half)
            for beams in pieces:
                nc.scalar.activation(t[:, beams], sums[i][half][:, beams], ACT.Square)
            squares[(i, half)] = t

        def add(i, beams=WHOLE):
            if i not in powers:
                power = finish.tile([P, BEAMS], F32, name="power")
                powers[i] = power
            nc.vector.tensor_tensor(
                out=powers[i][:, beams], in0=squares[(i, 0)][:, beams], in1=squares[(i, 1)][:, beams], op=ALU.add
            )

        def weigh(i, beams=WHOLE):
            if i not in stats:
                stat = finish.tile([P, BEAMS], F32, name="stat")
                stats[i] = stat
            nc.vector.tensor_tensor(
                out=stats[i][:, beams], in0=powers[i][:, beams], in1=noise[:, beams], op=ALU.mult
            )
            if i == TILES - 1:
                nc.sync.dma_start(out=stat_rows[:, i, beams], in_=stats[i][:, beams])
            elif beams.stop == BEAMS:
                nc.sync.dma_start(out=stat_rows[:, i, :], in_=stats[i][:])

        def strongest(i):
            nc.vector.tensor_reduce(
                out=peaks[:, i : i + 1], in_=stats[i][:], axis=mybir.AxisListType.X, op=ALU.max
            )

        def keep_busy(count):
            t = bank(7)
            for k in range(count):
                nc.tensor.matmul(t[:], lhsT=ones[:], rhs=zeros[:], start=True, stop=True)

        keep_busy(5)
        for i in (0, 1):
            for c in (0, 1):
                turn((i, c), 2 * i + c)
                collect((i, c))
                quantize((i, c))
            if i == 0:
                keep_busy(2)
        sums[0] = (bank(4), bank(5))
        sums[1] = (bank(6), bank(7))
        multiply_both(0, [0])
        multiply_both(1, [0])
        spread = bank(1)
        nc.tensor.matmul(spread[:], lhsT=ones[:], rhs=noise_row[:], start=True, stop=True)
        nc.scalar.copy(out=noise[:], in_=spread[:])
        multiply_both(0, [1])
        multiply_both(1, [1])

        chunks = ((2, 0), (2, 1), (3, 0), (3, 1))
        for chunk in chunks:
            lay_out(chunk)
        for chunk, b in zip(chunks, (2, 3, 0, 1)):
            turn(chunk, b)
            collect(chunk)
        for chunk in chunks:
            quantize(chunk)
        sums[2] = (bank(2), bank(3))
        multiply_both(2, [0, 1])
        for i in (0, 1, 2):
            multiply_both(i, [2])
        for chunk, b in (((0, 2), 0), ((2, 2), 1)):
            lay_out(chunk)
            turn(chunk, b)
            collect(chunk)
        for i in (0, 1, 2):
            multiply_both(i, [3])

        interleave_v(nc.vector.tensor_copy, 0, 0, 512)
        quantize_v(0)
        quantize((0, 2))
        quantize((2, 2))
        sums[3] = (bank(0), bank(1))
        multiply_both(3, [0, 1])
        interleave_v(nc.vector.tensor_copy, 1, 0, V_SPLIT)
        interleave_v(nc.scalar.copy, 1, V_SPLIT, 512)
        quantize_v(1)
        for i in (0, 1, 2):
            multiply(i, 0, AUX_PASS)
            square(i, 0)
        for i in (0, 1, 2):
            multiply(i, 1, AUX_PASS)

        for chunk in ((4, 0), (4, 1), (4, 2), (5, 0), (5, 1), (6, 0), (6, 1), (6, 2)):
            lay_out(chunk)
        for c, b in enumerate((4, 6, 2)):
            turn((4, c), b)
            square(c, 1)
            collect((4, c))
        multiply_both(3, [2, 3, AUX_PASS])
        add(0)
        quantize((4, 0))
        add(1)
        weigh(0)
        quantize((4, 1))
        add(2)
        quantize((4, 2))
        weigh(1)
        strongest(0)

        for chunk, b in (((5, 0), 5), ((5, 1), 7), ((6, 0), 3), ((6, 1), 4)):
            turn(chunk, b)
            collect(chunk)
        square(3, 0)
        square(3, 1)
        lay_out((7, 0))
        lay_out((7, 1))
        sums[4] = (bank(6), bank(2))
        multiply_both(4, range(5))
        quantize((5, 0))
        weigh(2)
        quantize((5, 1))
        strongest(1)
        quantize((6, 0))
        add(3)
        quantize((6, 1))
        strongest(2)
        weigh(3)

        for chunk, b in (((6, 2), 5), ((7, 0), 7), ((7, 1), 3)):
            turn(chunk, b)
            collect(chunk)
        square(4, 0)
        square(4, 1)
        sums[5] = (bank(0), bank(1))
        multiply_both(5, range(5))
        quantize((6, 2))
        strongest(3)
        quantize((7, 0))
        add(4)
        quantize((7, 1))
        weigh(4)
        square(5, 0)
        square(5, 1)
        sums[6] = (bank(6), bank(2))
        multiply_both(6, range(5))
        add(5, PIECES[0])
        strongest(4)
        add(5, PIECES[1])
        for beams in PIECES:
            weigh(5, beams)
        sums[7] = (bank(5), bank(4))
        for half in (0, 1):
            for g in range(5):
                multiply(7, half, g)
        square(6, 0)
        square(6, 1)
        strongest(5)
        for beams in PIECES:
            add(6, beams)
        for beams in PIECES:
            weigh(6, beams)
        square(7, 0)
        square(7, 1, PIECES)
        strongest(6)
        for beams in PIECES:
            add(7, beams)
        for beams in PIECES:
            weigh(7, beams)
        strongest(7)
        nc.sync.dma_start(out=peak_rows, in_=peaks[:])
